import numpy as np
import ml_dtypes


def mxq(x, axis, fmt="e4m3"):
    dtype, down = {"e4m3": (ml_dtypes.float8_e4m3fn, 7), "e5m2": (ml_dtypes.float8_e5m2, 14)}[fmt]
    v = np.moveaxis(np.asarray(x, np.float32).astype(ml_dtypes.bfloat16).astype(np.float64), axis, -1)
    blocks = v.reshape(v.shape[:-1] + (-1, 32))
    amax = np.abs(blocks).max(-1, keepdims=True)
    byte = np.maximum(np.where(amax > 0, np.frexp(amax)[1] - 1 + 127, 0) - down, 1)
    scale = np.exp2(byte - 127.0)
    codes = (blocks / scale).astype(np.float32).astype(dtype).astype(np.float64)
    return np.moveaxis((codes * scale).reshape(v.shape), -1, axis)


WIDE = False


def mx_kscale(k):
    if not WIDE:
        return np.ones(k)
    levels = np.array([10, -10, 5, -5, 0])
    if k % 512:
        return np.exp2(np.random.permutation(np.resize(levels, k // 32))).repeat(32)
    a = np.empty((k // 512, 16))
    for p in range(k // 512):
        a[p, :8] = np.random.permutation(np.resize(levels, 8))
        for g in range(8):
            far = levels[np.abs(levels - a[p, g]) >= 10]
            a[p, g + 8] = far[np.random.randint(len(far))]
    return np.exp2(a.ravel()).repeat(32)


def f64(x):
    return np.asarray(x).astype(np.float64)


def striped(idx):
    return np.tile(idx.reshape(-1, 16).T, (8, 1)).astype(np.uint16)


def unstriped(offs):
    return offs[:16].T.reshape(-1).astype(np.int64)


K, T, E, C, N = 2048, 1024, 2, 256, 512


def by_expert(wq, xq):
    return np.concatenate([wq[e].T @ xq[:, e * C:(e + 1) * C] for e in range(E)], axis=1)


def setup_inputs():
    n = np.random.standard_normal
    s = mx_kscale(K)[:, None]
    return {
        "xT": (n((K, T)) * s).astype(np.float32),
        "w": (n((E, K, N)) / np.sqrt(K) / s[None]).astype(np.float32),
        "gate": np.tile(np.random.uniform(0.2, 1.0, E * C), (N, 1)).astype(np.float32),
        "offs": striped(np.random.permutation(T)[:E * C]),
    }


def reference(xT, w, gate, offs):
    idx = unstriped(offs)
    xq = mxq(f64(xT)[:, idx], 0, "e4m3")
    y = by_expert(mxq(f64(w), 1, "e4m3"), xq)
    out = np.zeros((N, T))
    out[:, idx] = f64(gate) * y
    return out

@@ -1,0 +1,174 @@
+from contextlib import ExitStack
+
+import concourse.mybir as mybir
+
+K, T, E, C, N = 2048, 1024, 2, 256, 512
+FLOPS = 2 * K * N * E * C
+
+F32 = mybir.dt.float32
+BF16 = mybir.dt.bfloat16
+U32 = mybir.dt.uint32
+U16 = mybir.dt.uint16
+U8 = mybir.dt.uint8
+FP8X4 = mybir.dt.float8_e4m3fn_x4
+MULT = mybir.AluOpType.mult
+
+P = 128
+PACK = 4
+K_PASS = P * PACK
+PASSES = K // K_PASS
+NB = N // P
+SLOTS = E * C
+LIST_COLS = C // 16
+
+
+def tile_routed_moe_kernel(tc, xT, w, gate, offs, out):
+    nc = tc.nc
+    x_view = xT.rearrange("(g p t) n -> g p t n", p=P, t=PACK)
+    w_view = w.rearrange("e (g p j) n -> e g p j n", p=P, j=PACK)
+    gate_view = gate.rearrange("(b p) s -> p b s", p=P)
+
+    with ExitStack() as ctx:
+        keep = ctx.enter_context(tc.tile_pool(name="keep", bufs=1))
+        stage = ctx.enter_context(tc.tile_pool(name="stage", bufs=4))
+        psum = ctx.enter_context(tc.psum_pool(name="psum", bufs=1))
+
+        offsets = keep.tile([P, SLOTS // 16], U16, name="offsets")
+        nc.sync.dma_start(offsets[:], offs)
+
+        raw_x = [keep.tile([P, PACK, T], F32, name="raw_x%d" % g) for g in range(PASSES)]
+        raw_w = [[keep.tile([P, PACK, N], F32, name="raw_w%d%d" % (e, g)) for g in range(PASSES)] for e in range(E)]
+        gate_sb = keep.tile([P, NB, SLOTS], F32, name="gate_sb")
+
+        def load_x(g, pieces):
+            step = PACK // pieces
+            for t0 in range(0, PACK, step):
+                nc.sync.dma_start(raw_x[g][:, t0:t0 + step, :], x_view[g, :, t0:t0 + step, :])
+
+        def load_w(e, g):
+            nc.sync.dma_start(raw_w[e][g][:], w_view[e, g])
+
+        def load_gate(e):
+            nc.sync.dma_start(gate_sb[:, :, e * C:(e + 1) * C], gate_view[:, :, e * C:(e + 1) * C])
+
+        load_x(0, 4)
+        load_x(1, 2)
+        load_w(0, 0)
+        load_x(2, 2)
+        load_w(0, 1)
+        load_x(3, 2)
+        load_w(0, 2)
+        load_w(0, 3)
+        load_gate(0)
+        load_w(1, 0)
+        load_w(1, 1)
+        load_gate(1)
+        load_w(1, 2)
+        for b in range(NB):
+            nc.sync.dma_start(raw_w[1][3][:, :, b * P:(b + 1) * P], w_view[1, 3, :, :, b * P:(b + 1) * P])
+
+        windows = [keep.tile([P, T], F32, name="window%d" % b) for b in range(NB)]
+        for b in range(NB):
+            nc.gpsimd.memset(windows[b][:], 0.0)
+
+        x_codes = [keep.tile([P, SLOTS], U32, name="x_codes%d" % g, align_bytes=64) for g in range(PASSES)]
+        x_scales = [keep.tile([P, SLOTS], U8, name="x_scales%d" % g, align_bytes=64) for g in range(PASSES)]
+        w_codes = [[keep.tile([P, N], U32, name="w_codes%d%d" % (e, g), align_bytes=64) for g in range(PASSES)] for e in range(E)]
+        w_scales = [[keep.tile([P, N], U8, name="w_scales%d%d" % (e, g), align_bytes=64) for g in range(PASSES)] for e in range(E)]
+        acc = [[psum.tile([P, C], F32, name="acc%d%d" % (e, b)) for b in range(NB)] for e in range(E)]
+        sums = [[keep.tile([P, C], F32, name="sums%d%d" % (e, b)) for b in range(NB)] for e in range(E)]
+        x_grouped = {}
+        w_grouped = {}
+
+        def gather(g, t):
+            if t == 0:
+                x_grouped[g] = stage.tile([P, SLOTS, PACK], BF16, name="x_grouped", align_bytes=64)
+            nc.vector.tensor_copy(out=x_grouped[g][:, :, t], in_=raw_x[g][:, t, :].indirect(offsets[:]))
+
+        def quantize_x(g):
+            nc.vector.quantize_mx(
+                out=x_codes[g][:].bitcast(FP8X4),
+                scales=x_scales[g][:],
+                in_=x_grouped[g][:].rearrange("p c t -> p (c t)"),
+            )
+
+        def interleave_w(e, g, n0, n1):
+            if n0 == 0:
+                w_grouped[(e, g)] = stage.tile([P, N, PACK], BF16, name="w_grouped", align_bytes=64)
+            nc.scalar.copy(
+                out=w_grouped[(e, g)][:, n0:n1, :].rearrange("p (c i) j -> p c j i", i=4),
+                in_=raw_w[e][g][:, :, n0:n1].rearrange("p j (c i) -> p c j i", i=4),
+            )
+
+        def interleave_halves(e, g):
+            interleave_w(e, g, 0, N // 2)
+            interleave_w(e, g, N // 2, N)
+
+        def quantize_w(e, g, n0, n1):
+            nc.vector.quantize_mx(
+                out=w_codes[e][g][:, n0:n1].bitcast(FP8X4),
+                scales=w_scales[e][g][:, n0:n1],
+                in_=w_grouped[(e, g)][:].rearrange("p n j -> p (n j)")[:, n0 * PACK:n1 * PACK],
+            )
+
+        def multiply(e, g, b):
+            nc.tensor.matmul_mx(
+                out=acc[e][b][:],
+                lhsT=w_codes[e][g][:, b * P:(b + 1) * P].bitcast(FP8X4),
+                lhsT_scale=w_scales[e][g][:, b * P:(b + 1) * P],
+                rhs=x_codes[g][:, e * C:(e + 1) * C].bitcast(FP8X4),
+                rhs_scale=x_scales[g][:, e * C:(e + 1) * C],
+                start=(g == 0),
+                stop=(g == PASSES - 1),
+            )
+
+        def way_back(e, b):
+            nc.scalar.copy(out=sums[e][b][:], in_=acc[e][b][:])
+            nc.vector.tensor_tensor(
+                windows[b][:].indirect(offsets[:, e * LIST_COLS:(e + 1) * LIST_COLS]),
+                sums[e][b][:],
+                gate_sb[:, b, e * C:(e + 1) * C],
+                MULT,
+            )
+
+        def whole_chunk(e, g):
+            quantize_w(e, g, 0, N)
+            for b in range(NB):
+                multiply(e, g, b)
+
+        def last_chunk(e):
+            g = PASSES - 1
+            for b in range(NB):
+                interleave_w(e, g, b * P, (b + 1) * P)
+                quantize_w(e, g, b * P, (b + 1) * P)
+                multiply(e, g, b)
+                way_back(e, b)
+                if e == E - 1:
+                    nc.sync.dma_start(out[b * P:(b + 1) * P, :], windows[b][:])
+
+        for t in range(PACK):
+            gather(0, t)
+        gather(1, 0)
+        quantize_x(0)
+        for t in range(1, PACK):
+            gather(1, t)
+        interleave_halves(0, 0)
+        gather(2, 0)
+        quantize_x(1)
+        whole_chunk(0, 0)
+        for t in range(1, PACK):
+            gather(2, t)
+        interleave_halves(0, 1)
+        gather(3, 0)
+        quantize_x(2)
+        whole_chunk(0, 1)
+        for t in range(1, PACK):
+            gather(3, t)
+        interleave_halves(0, 2)
+        whole_chunk(0, 2)
+        quantize_x(3)
+        last_chunk(0)
+        for g in range(PASSES - 1):
+            interleave_halves(1, g)
+            whole_chunk(1, g)
+        last_chunk(1)

@@ -40,10 +40,11 @@ def tile_routed_moe_kernel(tc, xT, w, gate, offs, out):
         raw_w = [[keep.tile([P, PACK, N], F32, name="raw_w%d%d" % (e, g)) for g in range(PASSES)] for e in range(E)]
         gate_sb = keep.tile([P, NB, SLOTS], F32, name="gate_sb")
 
-        def load_x(g, pieces):
-            step = PACK // pieces
-            for t0 in range(0, PACK, step):
-                nc.sync.dma_start(raw_x[g][:, t0:t0 + step, :], x_view[g, :, t0:t0 + step, :])
+        def load_x(g, t0, t1):
+            nc.sync.dma_start(raw_x[g][:, t0:t1, :], x_view[g, :, t0:t1, :])
+
+        def load_w_block(e, g, b):
+            nc.sync.dma_start(raw_w[e][g][:, :, b * P:(b + 1) * P], w_view[e, g, :, :, b * P:(b + 1) * P])
 
         def load_w(e, g):
             nc.sync.dma_start(raw_w[e][g][:], w_view[e, g])
@@ -51,21 +52,25 @@ def tile_routed_moe_kernel(tc, xT, w, gate, offs, out):
         def load_gate(e):
             nc.sync.dma_start(gate_sb[:, :, e * C:(e + 1) * C], gate_view[:, :, e * C:(e + 1) * C])
 
-        load_x(0, 4)
-        load_x(1, 2)
+        for t in range(PACK):
+            load_x(0, t, t + 1)
+        load_x(1, 0, 2)
+        load_x(1, 2, 4)
         load_w(0, 0)
-        load_x(2, 2)
+        load_x(2, 0, 2)
+        load_x(2, 2, 4)
         load_w(0, 1)
-        load_x(3, 2)
+        load_x(3, 0, 2)
         load_w(0, 2)
+        load_x(3, 2, 4)
         load_w(0, 3)
         load_gate(0)
         load_w(1, 0)
         load_w(1, 1)
-        load_gate(1)
-        load_w(1, 2)
         for b in range(NB):
-            nc.sync.dma_start(raw_w[1][3][:, :, b * P:(b + 1) * P], w_view[1, 3, :, :, b * P:(b + 1) * P])
+            load_w_block(1, 2, b)
+            load_w_block(1, 3, b)
+        load_gate(1)
 
         windows = [keep.tile([P, T], F32, name="window%d" % b) for b in range(NB)]
         for b in range(NB):
@@ -92,17 +97,19 @@ def tile_routed_moe_kernel(tc, xT, w, gate, offs, out):
                 in_=x_grouped[g][:].rearrange("p c t -> p (c t)"),
             )
 
-        def interleave_w(e, g, n0, n1):
+        def interleave_w(e, g, n0, n1, on_vector=False):
             if n0 == 0:
                 w_grouped[(e, g)] = stage.tile([P, N, PACK], BF16, name="w_grouped", align_bytes=64)
-            nc.scalar.copy(
-                out=w_grouped[(e, g)][:, n0:n1, :].rearrange("p (c i) j -> p c j i", i=4),
-                in_=raw_w[e][g][:, :, n0:n1].rearrange("p j (c i) -> p c j i", i=4),
-            )
-
-        def interleave_halves(e, g):
-            interleave_w(e, g, 0, N // 2)
-            interleave_w(e, g, N // 2, N)
+            if on_vector:
+                nc.vector.tensor_copy(
+                    out=w_grouped[(e, g)][:, n0:n1, :],
+                    in_=raw_w[e][g][:, :, n0:n1].rearrange("p j n -> p n j"),
+                )
+            else:
+                nc.scalar.copy(
+                    out=w_grouped[(e, g)][:, n0:n1, :].rearrange("p (c i) j -> p c j i", i=4),
+                    in_=raw_w[e][g][:, :, n0:n1].rearrange("p j (c i) -> p c j i", i=4),
+                )
 
         def quantize_w(e, g, n0, n1):
             nc.vector.quantize_mx(
@@ -122,6 +129,18 @@ def tile_routed_moe_kernel(tc, xT, w, gate, offs, out):
                 stop=(g == PASSES - 1),
             )
 
+        def whole_chunk(e, g):
+            interleave_w(e, g, 0, N // 2)
+            interleave_w(e, g, N // 2, N)
+            quantize_w(e, g, 0, N)
+            for b in range(NB):
+                multiply(e, g, b)
+
+        def block_of_chunk(e, g, b, on_vector=False):
+            interleave_w(e, g, b * P, (b + 1) * P, on_vector)
+            quantize_w(e, g, b * P, (b + 1) * P)
+            multiply(e, g, b)
+
         def way_back(e, b):
             nc.scalar.copy(out=sums[e][b][:], in_=acc[e][b][:])
             nc.vector.tensor_tensor(
@@ -131,44 +150,33 @@ def tile_routed_moe_kernel(tc, xT, w, gate, offs, out):
                 MULT,
             )
 
-        def whole_chunk(e, g):
-            quantize_w(e, g, 0, N)
-            for b in range(NB):
-                multiply(e, g, b)
-
-        def last_chunk(e):
-            g = PASSES - 1
-            for b in range(NB):
-                interleave_w(e, g, b * P, (b + 1) * P)
-                quantize_w(e, g, b * P, (b + 1) * P)
-                multiply(e, g, b)
-                way_back(e, b)
-                if e == E - 1:
-                    nc.sync.dma_start(out[b * P:(b + 1) * P, :], windows[b][:])
-
         for t in range(PACK):
             gather(0, t)
         gather(1, 0)
         quantize_x(0)
         for t in range(1, PACK):
             gather(1, t)
-        interleave_halves(0, 0)
+        whole_chunk(0, 0)
         gather(2, 0)
         quantize_x(1)
-        whole_chunk(0, 0)
         for t in range(1, PACK):
             gather(2, t)
-        interleave_halves(0, 1)
+        whole_chunk(0, 1)
         gather(3, 0)
         quantize_x(2)
-        whole_chunk(0, 1)
         for t in range(1, PACK):
             gather(3, t)
-        interleave_halves(0, 2)
         whole_chunk(0, 2)
         quantize_x(3)
-        last_chunk(0)
-        for g in range(PASSES - 1):
-            interleave_halves(1, g)
-            whole_chunk(1, g)
-        last_chunk(1)
+        for b in range(NB):
+            block_of_chunk(0, 3, b)
+        for b in range(NB):
+            way_back(0, b)
+        whole_chunk(1, 0)
+        whole_chunk(1, 1)
+        for b in range(NB):
+            block_of_chunk(1, 2, b, on_vector=True)
+            block_of_chunk(1, 3, b)
+        for b in range(NB):
+            way_back(1, b)
+            nc.sync.dma_start(out[b * P:(b + 1) * P, :], windows[b][:])

@@ -12,6 +12,7 @@ U16 = mybir.dt.uint16
 U8 = mybir.dt.uint8
 FP8X4 = mybir.dt.float8_e4m3fn_x4
 MULT = mybir.AluOpType.mult
+COPY = mybir.ActivationFunctionType.Copy
 
 P = 128
 PACK = 4
@@ -20,6 +21,7 @@ PASSES = K // K_PASS
 NB = N // P
 SLOTS = E * C
 LIST_COLS = C // 16
+SCALAR_PASS = 1
 
 
 def tile_routed_moe_kernel(tc, xT, w, gate, offs, out):
@@ -39,36 +41,41 @@ def tile_routed_moe_kernel(tc, xT, w, gate, offs, out):
         raw_x = [keep.tile([P, PACK, T], F32, name="raw_x%d" % g) for g in range(PASSES)]
         raw_w = [[keep.tile([P, PACK, N], F32, name="raw_w%d%d" % (e, g)) for g in range(PASSES)] for e in range(E)]
         gate_sb = keep.tile([P, NB, SLOTS], F32, name="gate_sb")
+        x_bf16 = keep.tile([P, PACK, T], BF16, name="x_bf16")
 
         def load_x(g, t0, t1):
             nc.sync.dma_start(raw_x[g][:, t0:t1, :], x_view[g, :, t0:t1, :])
 
-        def load_w_block(e, g, b):
-            nc.sync.dma_start(raw_w[e][g][:, :, b * P:(b + 1) * P], w_view[e, g, :, :, b * P:(b + 1) * P])
-
         def load_w(e, g):
             nc.sync.dma_start(raw_w[e][g][:], w_view[e, g])
+
+        def load_w_block(e, g, b):
+            nc.sync.dma_start(raw_w[e][g][:, :, b * P:(b + 1) * P], w_view[e, g, :, :, b * P:(b + 1) * P])
 
         def load_gate(e):
             nc.sync.dma_start(gate_sb[:, :, e * C:(e + 1) * C], gate_view[:, :, e * C:(e + 1) * C])
 
-        for t in range(PACK):
-            load_x(0, t, t + 1)
-        load_x(1, 0, 2)
-        load_x(1, 2, 4)
-        load_w(0, 0)
+        load_x(0, 0, 1)
+        load_x(0, 1, 2)
+        load_x(1, 0, 1)
+        load_x(0, 2, 3)
+        load_x(0, 3, 4)
+        load_x(1, 1, 2)
         load_x(2, 0, 2)
+        load_x(1, 2, 3)
         load_x(2, 2, 4)
-        load_w(0, 1)
+        load_x(1, 3, 4)
         load_x(3, 0, 2)
-        load_w(0, 2)
+        load_w(0, 0)
         load_x(3, 2, 4)
+        load_w(0, 1)
+        load_w(0, 2)
         load_w(0, 3)
         load_gate(0)
         load_w(1, 0)
         load_w(1, 1)
+        load_w(1, 2)
         for b in range(NB):
-            load_w_block(1, 2, b)
             load_w_block(1, 3, b)
         load_gate(1)
 
@@ -82,13 +89,20 @@ def tile_routed_moe_kernel(tc, xT, w, gate, offs, out):
         w_scales = [[keep.tile([P, N], U8, name="w_scales%d%d" % (e, g), align_bytes=64) for g in range(PASSES)] for e in range(E)]
         acc = [[psum.tile([P, C], F32, name="acc%d%d" % (e, b)) for b in range(NB)] for e in range(E)]
         sums = [[keep.tile([P, C], F32, name="sums%d%d" % (e, b)) for b in range(NB)] for e in range(E)]
-        x_grouped = {}
+        x_grouped = [stage.tile([P, SLOTS, PACK], BF16, name="x_grouped", align_bytes=64) for g in range(PASSES)]
         w_grouped = {}
 
         def gather(g, t):
-            if t == 0:
-                x_grouped[g] = stage.tile([P, SLOTS, PACK], BF16, name="x_grouped", align_bytes=64)
-            nc.vector.tensor_copy(out=x_grouped[g][:, :, t], in_=raw_x[g][:, t, :].indirect(offsets[:]))
+            if g == SCALAR_PASS:
+                nc.scalar.copy(out=x_bf16[:, t, :], in_=raw_x[g][:, t, :])
+                for e in range(E):
+                    nc.scalar.activation(
+                        x_grouped[g][:, e * C:(e + 1) * C, t],
+                        x_bf16[:, t, :].indirect(offsets[:, e * LIST_COLS:(e + 1) * LIST_COLS]),
+                        COPY,
+                    )
+            else:
+                nc.vector.tensor_copy(out=x_grouped[g][:, :, t], in_=raw_x[g][:, t, :].indirect(offsets[:]))
 
         def quantize_x(g):
             nc.vector.quantize_mx(
@@ -97,19 +111,13 @@ def tile_routed_moe_kernel(tc, xT, w, gate, offs, out):
                 in_=x_grouped[g][:].rearrange("p c t -> p (c t)"),
             )
 
-        def interleave_w(e, g, n0, n1, on_vector=False):
+        def interleave_w(e, g, n0, n1):
             if n0 == 0:
                 w_grouped[(e, g)] = stage.tile([P, N, PACK], BF16, name="w_grouped", align_bytes=64)
-            if on_vector:
-                nc.vector.tensor_copy(
-                    out=w_grouped[(e, g)][:, n0:n1, :],
-                    in_=raw_w[e][g][:, :, n0:n1].rearrange("p j n -> p n j"),
-                )
-            else:
-                nc.scalar.copy(
-                    out=w_grouped[(e, g)][:, n0:n1, :].rearrange("p (c i) j -> p c j i", i=4),
-                    in_=raw_w[e][g][:, :, n0:n1].rearrange("p j (c i) -> p c j i", i=4),
-                )
+            nc.scalar.copy(
+                out=w_grouped[(e, g)][:, n0:n1, :].rearrange("p (c i) j -> p c j i", i=4),
+                in_=raw_w[e][g][:, :, n0:n1].rearrange("p j (c i) -> p c j i", i=4),
+            )
 
         def quantize_w(e, g, n0, n1):
             nc.vector.quantize_mx(
@@ -136,8 +144,8 @@ def tile_routed_moe_kernel(tc, xT, w, gate, offs, out):
             for b in range(NB):
                 multiply(e, g, b)
 
-        def block_of_chunk(e, g, b, on_vector=False):
-            interleave_w(e, g, b * P, (b + 1) * P, on_vector)
+        def block_of_chunk(e, g, b):
+            interleave_w(e, g, b * P, (b + 1) * P)
             quantize_w(e, g, b * P, (b + 1) * P)
             multiply(e, g, b)
 
@@ -149,34 +157,34 @@ def tile_routed_moe_kernel(tc, xT, w, gate, offs, out):
                 gate_sb[:, b, e * C:(e + 1) * C],
                 MULT,
             )
+            if e == E - 1:
+                nc.sync.dma_start(out[b * P:(b + 1) * P, :], windows[b][:])
+
+        def last_chunk(e):
+            g = PASSES - 1
+            block_of_chunk(e, g, 0)
+            for b in range(1, NB):
+                block_of_chunk(e, g, b)
+                way_back(e, b - 1)
+            way_back(e, NB - 1)
 
         for t in range(PACK):
             gather(0, t)
-        gather(1, 0)
+            gather(1, t)
+        gather(2, 0)
         quantize_x(0)
         for t in range(1, PACK):
-            gather(1, t)
-        whole_chunk(0, 0)
-        gather(2, 0)
-        quantize_x(1)
-        for t in range(1, PACK):
             gather(2, t)
-        whole_chunk(0, 1)
         gather(3, 0)
         quantize_x(2)
+        quantize_x(1)
         for t in range(1, PACK):
             gather(3, t)
-        whole_chunk(0, 2)
+        whole_chunk(0, 0)
         quantize_x(3)
-        for b in range(NB):
-            block_of_chunk(0, 3, b)
-        for b in range(NB):
-            way_back(0, b)
-        whole_chunk(1, 0)
-        whole_chunk(1, 1)
-        for b in range(NB):
-            block_of_chunk(1, 2, b, on_vector=True)
-            block_of_chunk(1, 3, b)
-        for b in range(NB):
-            way_back(1, b)
-            nc.sync.dma_start(out[b * P:(b + 1) * P, :], windows[b][:])
+        whole_chunk(0, 1)
+        whole_chunk(0, 2)
+        last_chunk(0)
+        for g in range(PASSES - 1):
+            whole_chunk(1, g)
+        last_chunk(1)

@@ -111,9 +111,15 @@ def tile_routed_moe_kernel(tc, xT, w, gate, offs, out):
                 in_=x_grouped[g][:].rearrange("p c t -> p (c t)"),
             )
 
-        def interleave_w(e, g, n0, n1):
+        def interleave_w(e, g, n0, n1, on_vector=False):
             if n0 == 0:
                 w_grouped[(e, g)] = stage.tile([P, N, PACK], BF16, name="w_grouped", align_bytes=64)
+            if on_vector:
+                nc.vector.tensor_copy(
+                    out=w_grouped[(e, g)][:, n0:n1, :],
+                    in_=raw_w[e][g][:, :, n0:n1].rearrange("p j n -> p n j"),
+                )
+                return
             nc.scalar.copy(
                 out=w_grouped[(e, g)][:, n0:n1, :].rearrange("p (c i) j -> p c j i", i=4),
                 in_=raw_w[e][g][:, :, n0:n1].rearrange("p j (c i) -> p c j i", i=4),
@@ -185,6 +191,14 @@ def tile_routed_moe_kernel(tc, xT, w, gate, offs, out):
         whole_chunk(0, 1)
         whole_chunk(0, 2)
         last_chunk(0)
-        for g in range(PASSES - 1):
-            whole_chunk(1, g)
+        for g in (0, 1):
+            interleave_w(1, g, 0, N)
+            quantize_w(1, g, 0, N)
+            for b in range(NB):
+                multiply(1, g, b)
+        interleave_w(1, 2, 0, N // 2)
+        interleave_w(1, 2, N // 2, N, on_vector=True)
+        quantize_w(1, 2, 0, N)
+        for b in range(NB):
+            multiply(1, 2, b)
         last_chunk(1)

@@ -94,7 +94,7 @@ def tile_routed_moe_kernel(tc, xT, w, gate, offs, out):
 
         def gather(g, t):
             if g == SCALAR_PASS:
-                nc.scalar.copy(out=x_bf16[:, t, :], in_=raw_x[g][:, t, :])
+                nc.gpsimd.tensor_copy(out=x_bf16[:, t, :], in_=raw_x[g][:, t, :])
                 for e in range(E):
                     nc.scalar.activation(
                         x_grouped[g][:, e * C:(e + 1) * C, t],

@@ -81,7 +81,7 @@ def tile_routed_moe_kernel(tc, xT, w, gate, offs, out):
 
         windows = [keep.tile([P, T], F32, name="window%d" % b) for b in range(NB)]
         for b in range(NB):
-            nc.gpsimd.memset(windows[b][:], 0.0)
+            nc.vector.memset(windows[b][:], 0.0)
 
         x_codes = [keep.tile([P, SLOTS], U32, name="x_codes%d" % g, align_bytes=64) for g in range(PASSES)]
         x_scales = [keep.tile([P, SLOTS], U8, name="x_scales%d" % g, align_bytes=64) for g in range(PASSES)]

@@ -21,7 +21,7 @@ PASSES = K // K_PASS
 NB = N // P
 SLOTS = E * C
 LIST_COLS = C // 16
-SCALAR_PASS = 1
+SCALAR_PLANES = ((1, 0), (1, 1), (1, 2), (1, 3), (2, 2), (2, 3))
 
 
 def tile_routed_moe_kernel(tc, xT, w, gate, offs, out):
@@ -41,7 +41,6 @@ def tile_routed_moe_kernel(tc, xT, w, gate, offs, out):
         raw_x = [keep.tile([P, PACK, T], F32, name="raw_x%d" % g) for g in range(PASSES)]
         raw_w = [[keep.tile([P, PACK, N], F32, name="raw_w%d%d" % (e, g)) for g in range(PASSES)] for e in range(E)]
         gate_sb = keep.tile([P, NB, SLOTS], F32, name="gate_sb")
-        x_bf16 = keep.tile([P, PACK, T], BF16, name="x_bf16")
 
         def load_x(g, t0, t1):
             nc.sync.dma_start(raw_x[g][:, t0:t1, :], x_view[g, :, t0:t1, :])
@@ -49,25 +48,19 @@ def tile_routed_moe_kernel(tc, xT, w, gate, offs, out):
         def load_w(e, g):
             nc.sync.dma_start(raw_w[e][g][:], w_view[e, g])
 
-        def load_w_block(e, g, b):
-            nc.sync.dma_start(raw_w[e][g][:, :, b * P:(b + 1) * P], w_view[e, g, :, :, b * P:(b + 1) * P])
-
         def load_gate(e):
             nc.sync.dma_start(gate_sb[:, :, e * C:(e + 1) * C], gate_view[:, :, e * C:(e + 1) * C])
 
         load_x(0, 0, 1)
         load_x(0, 1, 2)
-        load_x(1, 0, 1)
-        load_x(0, 2, 3)
-        load_x(0, 3, 4)
-        load_x(1, 1, 2)
+        load_x(0, 2, 4)
+        load_x(1, 0, 2)
         load_x(2, 0, 2)
-        load_x(1, 2, 3)
-        load_x(2, 2, 4)
-        load_x(1, 3, 4)
+        load_x(1, 2, 4)
         load_x(3, 0, 2)
-        load_w(0, 0)
+        load_x(2, 2, 4)
         load_x(3, 2, 4)
+        load_w(0, 0)
         load_w(0, 1)
         load_w(0, 2)
         load_w(0, 3)
@@ -75,8 +68,7 @@ def tile_routed_moe_kernel(tc, xT, w, gate, offs, out):
         load_w(1, 0)
         load_w(1, 1)
         load_w(1, 2)
-        for b in range(NB):
-            load_w_block(1, 3, b)
+        load_w(1, 3)
         load_gate(1)
 
         windows = [keep.tile([P, T], F32, name="window%d" % b) for b in range(NB)]
@@ -85,22 +77,18 @@ def tile_routed_moe_kernel(tc, xT, w, gate, offs, out):
 
         x_codes = [keep.tile([P, SLOTS], U32, name="x_codes%d" % g, align_bytes=64) for g in range(PASSES)]
         x_scales = [keep.tile([P, SLOTS], U8, name="x_scales%d" % g, align_bytes=64) for g in range(PASSES)]
+        x_grouped = [keep.tile([P, SLOTS, PACK], BF16, name="x_grouped%d" % g, align_bytes=64) for g in range(PASSES)]
         w_codes = [[keep.tile([P, N], U32, name="w_codes%d%d" % (e, g), align_bytes=64) for g in range(PASSES)] for e in range(E)]
         w_scales = [[keep.tile([P, N], U8, name="w_scales%d%d" % (e, g), align_bytes=64) for g in range(PASSES)] for e in range(E)]
         acc = [[psum.tile([P, C], F32, name="acc%d%d" % (e, b)) for b in range(NB)] for e in range(E)]
         sums = [[keep.tile([P, C], F32, name="sums%d%d" % (e, b)) for b in range(NB)] for e in range(E)]
-        x_grouped = [stage.tile([P, SLOTS, PACK], BF16, name="x_grouped", align_bytes=64) for g in range(PASSES)]
         w_grouped = {}
 
         def gather(g, t):
-            if g == SCALAR_PASS:
-                nc.gpsimd.tensor_copy(out=x_bf16[:, t, :], in_=raw_x[g][:, t, :])
-                for e in range(E):
-                    nc.scalar.activation(
-                        x_grouped[g][:, e * C:(e + 1) * C, t],
-                        x_bf16[:, t, :].indirect(offsets[:, e * LIST_COLS:(e + 1) * LIST_COLS]),
-                        COPY,
-                    )
+            if (g, t) in SCALAR_PLANES:
+                cast = stage.tile([P, T], BF16, name="x_bf16")
+                nc.gpsimd.tensor_copy(out=cast[:], in_=raw_x[g][:, t, :])
+                nc.scalar.activation(x_grouped[g][:, :, t], cast[:].indirect(offsets[:]), COPY)
             else:
                 nc.vector.tensor_copy(out=x_grouped[g][:, :, t], in_=raw_x[g][:, t, :].indirect(offsets[:]))
 
@@ -111,49 +99,36 @@ def tile_routed_moe_kernel(tc, xT, w, gate, offs, out):
                 in_=x_grouped[g][:].rearrange("p c t -> p (c t)"),
             )
 
-        def interleave_w(e, g, n0, n1, on_vector=False):
-            if n0 == 0:
+        def piece(e, g, b0, b1, engine):
+            n0, n1 = b0 * P, b1 * P
+            if b0 == 0:
                 w_grouped[(e, g)] = stage.tile([P, N, PACK], BF16, name="w_grouped", align_bytes=64)
-            if on_vector:
+            grouped = w_grouped[(e, g)]
+            if engine == "V":
                 nc.vector.tensor_copy(
-                    out=w_grouped[(e, g)][:, n0:n1, :],
+                    out=grouped[:, n0:n1, :],
                     in_=raw_w[e][g][:, :, n0:n1].rearrange("p j n -> p n j"),
                 )
-                return
-            nc.scalar.copy(
-                out=w_grouped[(e, g)][:, n0:n1, :].rearrange("p (c i) j -> p c j i", i=4),
-                in_=raw_w[e][g][:, :, n0:n1].rearrange("p j (c i) -> p c j i", i=4),
-            )
-
-        def quantize_w(e, g, n0, n1):
+            else:
+                nc.scalar.copy(
+                    out=grouped[:, n0:n1, :].rearrange("p (c i) j -> p c j i", i=4),
+                    in_=raw_w[e][g][:, :, n0:n1].rearrange("p j (c i) -> p c j i", i=4),
+                )
             nc.vector.quantize_mx(
                 out=w_codes[e][g][:, n0:n1].bitcast(FP8X4),
                 scales=w_scales[e][g][:, n0:n1],
-                in_=w_grouped[(e, g)][:].rearrange("p n j -> p (n j)")[:, n0 * PACK:n1 * PACK],
+                in_=grouped[:].rearrange("p n j -> p (n j)")[:, n0 * PACK:n1 * PACK],
             )
-
-        def multiply(e, g, b):
-            nc.tensor.matmul_mx(
-                out=acc[e][b][:],
-                lhsT=w_codes[e][g][:, b * P:(b + 1) * P].bitcast(FP8X4),
-                lhsT_scale=w_scales[e][g][:, b * P:(b + 1) * P],
-                rhs=x_codes[g][:, e * C:(e + 1) * C].bitcast(FP8X4),
-                rhs_scale=x_scales[g][:, e * C:(e + 1) * C],
-                start=(g == 0),
-                stop=(g == PASSES - 1),
-            )
-
-        def whole_chunk(e, g):
-            interleave_w(e, g, 0, N // 2)
-            interleave_w(e, g, N // 2, N)
-            quantize_w(e, g, 0, N)
-            for b in range(NB):
-                multiply(e, g, b)
-
-        def block_of_chunk(e, g, b):
-            interleave_w(e, g, b * P, (b + 1) * P)
-            quantize_w(e, g, b * P, (b + 1) * P)
-            multiply(e, g, b)
+            for b in range(b0, b1):
+                nc.tensor.matmul_mx(
+                    out=acc[e][b][:],
+                    lhsT=w_codes[e][g][:, b * P:(b + 1) * P].bitcast(FP8X4),
+                    lhsT_scale=w_scales[e][g][:, b * P:(b + 1) * P],
+                    rhs=x_codes[g][:, e * C:(e + 1) * C].bitcast(FP8X4),
+                    rhs_scale=x_scales[g][:, e * C:(e + 1) * C],
+                    start=(g == 0),
+                    stop=(g == PASSES - 1),
+                )
 
         def way_back(e, b):
             nc.scalar.copy(out=sums[e][b][:], in_=acc[e][b][:])
@@ -166,39 +141,47 @@ def tile_routed_moe_kernel(tc, xT, w, gate, offs, out):
             if e == E - 1:
                 nc.sync.dma_start(out[b * P:(b + 1) * P, :], windows[b][:])
 
-        def last_chunk(e):
-            g = PASSES - 1
-            block_of_chunk(e, g, 0)
-            for b in range(1, NB):
-                block_of_chunk(e, g, b)
-                way_back(e, b - 1)
-            way_back(e, NB - 1)
-
-        for t in range(PACK):
-            gather(0, t)
-            gather(1, t)
-        gather(2, 0)
+        gather(0, 0)
+        gather(0, 1)
+        gather(0, 2)
+        gather(0, 3)
         quantize_x(0)
-        for t in range(1, PACK):
-            gather(2, t)
-        gather(3, 0)
-        quantize_x(2)
+        gather(1, 0)
+        gather(1, 1)
+        gather(2, 0)
+        gather(2, 1)
+        gather(1, 2)
+        gather(1, 3)
         quantize_x(1)
-        for t in range(1, PACK):
-            gather(3, t)
-        whole_chunk(0, 0)
+        gather(3, 0)
+        gather(3, 1)
+        gather(2, 2)
+        gather(2, 3)
+        quantize_x(2)
+        gather(3, 2)
+        gather(3, 3)
         quantize_x(3)
-        whole_chunk(0, 1)
-        whole_chunk(0, 2)
-        last_chunk(0)
-        for g in (0, 1):
-            interleave_w(1, g, 0, N)
-            quantize_w(1, g, 0, N)
-            for b in range(NB):
-                multiply(1, g, b)
-        interleave_w(1, 2, 0, N // 2)
-        interleave_w(1, 2, N // 2, N, on_vector=True)
-        quantize_w(1, 2, 0, N)
-        for b in range(NB):
-            multiply(1, 2, b)
-        last_chunk(1)
+        piece(0, 0, 0, 4, "S")
+        piece(0, 1, 0, 4, "S")
+        piece(0, 2, 0, 1, "V")
+        piece(0, 2, 1, 2, "S")
+        piece(0, 2, 2, 4, "S")
+        piece(0, 3, 0, 1, "V")
+        piece(0, 3, 1, 2, "S")
+        way_back(0, 0)
+        piece(0, 3, 2, 3, "V")
+        way_back(0, 1)
+        piece(0, 3, 3, 4, "S")
+        way_back(0, 2)
+        way_back(0, 3)
+        piece(1, 0, 0, 4, "S")
+        piece(1, 1, 0, 4, "S")
+        piece(1, 2, 0, 2, "S")
+        piece(1, 2, 2, 4, "S")
+        piece(1, 3, 0, 1, "V")
+        piece(1, 3, 1, 2, "S")
+        way_back(1, 0)
+        piece(1, 3, 2, 4, "S")
+        way_back(1, 1)
+        way_back(1, 2)
+        way_back(1, 3)

@@ -38,9 +38,9 @@ def tile_routed_moe_kernel(tc, xT, w, gate, offs, out):
         offsets = keep.tile([P, SLOTS // 16], U16, name="offsets")
         nc.sync.dma_start(offsets[:], offs)
 
-        raw_x = [keep.tile([P, PACK, T], F32, name="raw_x%d" % g) for g in range(PASSES)]
-        raw_w = [[keep.tile([P, PACK, N], F32, name="raw_w%d%d" % (e, g)) for g in range(PASSES)] for e in range(E)]
-        gate_sb = keep.tile([P, NB, SLOTS], F32, name="gate_sb")
+        raw_x = [keep.tile([P, PACK, T], F32, name="raw_x%d" % g, align_bytes=256) for g in range(PASSES)]
+        raw_w = [[keep.tile([P, PACK, N], F32, name="raw_w%d%d" % (e, g), align_bytes=256) for g in range(PASSES)] for e in range(E)]
+        gate_sb = keep.tile([P, NB, SLOTS], F32, name="gate_sb", align_bytes=256)
 
         def load_x(g, t0, t1):
             nc.sync.dma_start(raw_x[g][:, t0:t1, :], x_view[g, :, t0:t1, :])
@@ -71,7 +71,7 @@ def tile_routed_moe_kernel(tc, xT, w, gate, offs, out):
         load_w(1, 3)
         load_gate(1)
 
-        windows = [keep.tile([P, T], F32, name="window%d" % b) for b in range(NB)]
+        windows = [keep.tile([P, T], F32, name="window%d" % b, align_bytes=256) for b in range(NB)]
         for b in range(NB):
             nc.vector.memset(windows[b][:], 0.0)
 

@@ -22,6 +22,8 @@ NB = N // P
 SLOTS = E * C
 LIST_COLS = C // 16
 SCALAR_PLANES = ((1, 0), (1, 1), (1, 2), (1, 3), (2, 2), (2, 3))
+HALF = N // 2
+PAIR = 2
 
 
 def tile_routed_moe_kernel(tc, xT, w, gate, offs, out):
@@ -39,37 +41,48 @@ def tile_routed_moe_kernel(tc, xT, w, gate, offs, out):
         nc.sync.dma_start(offsets[:], offs)
 
         raw_x = [keep.tile([P, PACK, T], F32, name="raw_x%d" % g, align_bytes=256) for g in range(PASSES)]
-        raw_w = [[keep.tile([P, PACK, N], F32, name="raw_w%d%d" % (e, g), align_bytes=256) for g in range(PASSES)] for e in range(E)]
+        raw_w = [keep.tile([P, PACK, N], F32, name="raw_w%d" % g, align_bytes=256) for g in range(PASSES)]
+        raw_half = {}
         gate_sb = keep.tile([P, NB, SLOTS], F32, name="gate_sb", align_bytes=256)
 
         def load_x(g, t0, t1):
             nc.sync.dma_start(raw_x[g][:, t0:t1, :], x_view[g, :, t0:t1, :])
 
-        def load_w(e, g):
-            nc.sync.dma_start(raw_w[e][g][:], w_view[e, g])
+        def load_w(g):
+            nc.sync.dma_start(raw_w[g][:], w_view[0, g])
 
-        def load_gate(e):
-            nc.sync.dma_start(gate_sb[:, :, e * C:(e + 1) * C], gate_view[:, :, e * C:(e + 1) * C])
+        def load_half(h, q):
+            raw = keep.tile([P, PAIR, PACK, HALF], F32, name="raw_half%d%d" % (h, q), tag="raw_half%d%d" % (h, q), align_bytes=256)
+            for i in range(PAIR):
+                nc.sync.dma_start(raw[:, i, :, :], w_view[1, q * PAIR + i, :, :, h * HALF:(h + 1) * HALF])
+            raw_half[(h, q)] = raw
+
+        def load_gate(e, b0, b1):
+            nc.sync.dma_start(gate_sb[:, b0:b1, e * C:(e + 1) * C], gate_view[:, b0:b1, e * C:(e + 1) * C])
 
         load_x(0, 0, 1)
         load_x(0, 1, 2)
-        load_x(0, 2, 4)
-        load_x(1, 0, 2)
+        load_x(1, 0, 1)
+        load_x(0, 2, 3)
+        load_x(0, 3, 4)
+        load_x(1, 1, 2)
         load_x(2, 0, 2)
         load_x(1, 2, 4)
         load_x(3, 0, 2)
         load_x(2, 2, 4)
         load_x(3, 2, 4)
-        load_w(0, 0)
-        load_w(0, 1)
-        load_w(0, 2)
-        load_w(0, 3)
-        load_gate(0)
-        load_w(1, 0)
-        load_w(1, 1)
-        load_w(1, 2)
-        load_w(1, 3)
-        load_gate(1)
+        load_w(0)
+        load_w(1)
+        load_w(2)
+        load_w(3)
+        load_gate(0, 0, 2)
+        load_half(0, 0)
+        load_half(0, 1)
+        load_gate(0, 2, 4)
+        load_half(1, 0)
+        load_half(1, 1)
+        load_gate(1, 0, 1)
+        load_gate(1, 1, 4)
 
         windows = [keep.tile([P, T], F32, name="window%d" % b, align_bytes=256) for b in range(NB)]
         for b in range(NB):
@@ -78,15 +91,14 @@ def tile_routed_moe_kernel(tc, xT, w, gate, offs, out):
         x_codes = [keep.tile([P, SLOTS], U32, name="x_codes%d" % g, align_bytes=64) for g in range(PASSES)]
         x_scales = [keep.tile([P, SLOTS], U8, name="x_scales%d" % g, align_bytes=64) for g in range(PASSES)]
         x_grouped = [keep.tile([P, SLOTS, PACK], BF16, name="x_grouped%d" % g, align_bytes=64) for g in range(PASSES)]
-        w_codes = [[keep.tile([P, N], U32, name="w_codes%d%d" % (e, g), align_bytes=64) for g in range(PASSES)] for e in range(E)]
-        w_scales = [[keep.tile([P, N], U8, name="w_scales%d%d" % (e, g), align_bytes=64) for g in range(PASSES)] for e in range(E)]
+        w_codes = [keep.tile([P, N], U32, name="w_codes%d" % g, align_bytes=64) for g in range(PASSES)]
+        w_scales = [keep.tile([P, N], U8, name="w_scales%d" % g, align_bytes=64) for g in range(PASSES)]
         acc = [[psum.tile([P, C], F32, name="acc%d%d" % (e, b)) for b in range(NB)] for e in range(E)]
-        sums = [[keep.tile([P, C], F32, name="sums%d%d" % (e, b)) for b in range(NB)] for e in range(E)]
         w_grouped = {}
 
         def gather(g, t):
             if (g, t) in SCALAR_PLANES:
-                cast = stage.tile([P, T], BF16, name="x_bf16")
+                cast = stage.tile([P, T], BF16, name="x_bf16", bufs=3)
                 nc.gpsimd.tensor_copy(out=cast[:], in_=raw_x[g][:, t, :])
                 nc.scalar.activation(x_grouped[g][:, :, t], cast[:].indirect(offsets[:]), COPY)
             else:
@@ -99,54 +111,80 @@ def tile_routed_moe_kernel(tc, xT, w, gate, offs, out):
                 in_=x_grouped[g][:].rearrange("p c t -> p (c t)"),
             )
 
-        def piece(e, g, b0, b1, engine):
+        def multiply(e, g, b, codes, scales):
+            nc.tensor.matmul_mx(
+                out=acc[e][b][:],
+                lhsT=codes.bitcast(FP8X4),
+                lhsT_scale=scales,
+                rhs=x_codes[g][:, e * C:(e + 1) * C].bitcast(FP8X4),
+                rhs_scale=x_scales[g][:, e * C:(e + 1) * C],
+                start=(g == 0),
+                stop=(g == PASSES - 1),
+            )
+
+        def piece(g, b0, b1, engine):
             n0, n1 = b0 * P, b1 * P
             if b0 == 0:
-                w_grouped[(e, g)] = stage.tile([P, N, PACK], BF16, name="w_grouped", align_bytes=64)
-            grouped = w_grouped[(e, g)]
+                w_grouped[g] = stage.tile([P, N, PACK], BF16, name="w_grouped", tag="grouped%d" % N, bufs=3, align_bytes=64)
+            grouped = w_grouped[g]
             if engine == "V":
                 nc.vector.tensor_copy(
                     out=grouped[:, n0:n1, :],
-                    in_=raw_w[e][g][:, :, n0:n1].rearrange("p j n -> p n j"),
+                    in_=raw_w[g][:, :, n0:n1].rearrange("p j n -> p n j"),
                 )
             else:
                 nc.scalar.copy(
                     out=grouped[:, n0:n1, :].rearrange("p (c i) j -> p c j i", i=4),
-                    in_=raw_w[e][g][:, :, n0:n1].rearrange("p j (c i) -> p c j i", i=4),
+                    in_=raw_w[g][:, :, n0:n1].rearrange("p j (c i) -> p c j i", i=4),
                 )
             nc.vector.quantize_mx(
-                out=w_codes[e][g][:, n0:n1].bitcast(FP8X4),
-                scales=w_scales[e][g][:, n0:n1],
+                out=w_codes[g][:, n0:n1].bitcast(FP8X4),
+                scales=w_scales[g][:, n0:n1],
                 in_=grouped[:].rearrange("p n j -> p (n j)")[:, n0 * PACK:n1 * PACK],
             )
             for b in range(b0, b1):
-                nc.tensor.matmul_mx(
-                    out=acc[e][b][:],
-                    lhsT=w_codes[e][g][:, b * P:(b + 1) * P].bitcast(FP8X4),
-                    lhsT_scale=w_scales[e][g][:, b * P:(b + 1) * P],
-                    rhs=x_codes[g][:, e * C:(e + 1) * C].bitcast(FP8X4),
-                    rhs_scale=x_scales[g][:, e * C:(e + 1) * C],
-                    start=(g == 0),
-                    stop=(g == PASSES - 1),
-                )
+                multiply(0, g, b, w_codes[g][:, b * P:(b + 1) * P], w_scales[g][:, b * P:(b + 1) * P])
 
-        def way_back(e, b):
-            nc.scalar.copy(out=sums[e][b][:], in_=acc[e][b][:])
-            nc.vector.tensor_tensor(
-                windows[b][:].indirect(offsets[:, e * LIST_COLS:(e + 1) * LIST_COLS]),
-                sums[e][b][:],
-                gate_sb[:, b, e * C:(e + 1) * C],
-                MULT,
+        def half_piece(h, q, c0, c1):
+            width = c1 - c0
+            raw = raw_half[(h, q)]
+            grouped = stage.tile([P, PAIR, width, PACK], BF16, name="half_grouped", tag="grouped%d" % (PAIR * width), bufs=3, align_bytes=64)
+            codes = keep.tile([P, PAIR, width], U32, name="half_codes%d%d%d" % (h, q, c0), align_bytes=64)
+            scales = keep.tile([P, PAIR, width], U8, name="half_scales%d%d%d" % (h, q, c0), align_bytes=64)
+            nc.scalar.copy(
+                out=grouped[:].rearrange("p g (c i) j -> p g c j i", i=4),
+                in_=raw[:, :, :, c0:c1].rearrange("p g j (c i) -> p g c j i", i=4),
             )
-            if e == E - 1:
-                nc.sync.dma_start(out[b * P:(b + 1) * P, :], windows[b][:])
+            nc.vector.quantize_mx(
+                out=codes[:].rearrange("p g n -> p (g n)").bitcast(FP8X4),
+                scales=scales[:].rearrange("p g n -> p (g n)"),
+                in_=grouped[:].rearrange("p g n j -> p (g n j)"),
+            )
+            for f0 in range(0, width, P):
+                b = (h * HALF + c0 + f0) // P
+                for i in range(PAIR):
+                    multiply(1, q * PAIR + i, b, codes[:, i, f0:f0 + P], scales[:, i, f0:f0 + P])
+
+        def way_back(e, blocks, slot=None):
+            name = "sums%d%d" % (e, blocks[0])
+            sums = keep.tile([P, len(blocks), C], F32, name=name, tag=slot or name, align_bytes=256)
+            for k, b in enumerate(blocks):
+                nc.scalar.copy(out=sums[:, k, :], in_=acc[e][b][:])
+                nc.vector.tensor_tensor(
+                    windows[b][:].indirect(offsets[:, e * LIST_COLS:(e + 1) * LIST_COLS]),
+                    sums[:, k, :],
+                    gate_sb[:, b, e * C:(e + 1) * C],
+                    MULT,
+                )
+                if e == E - 1:
+                    nc.sync.dma_start(out[b * P:(b + 1) * P, :], windows[b][:])
 
         gather(0, 0)
         gather(0, 1)
+        gather(1, 0)
         gather(0, 2)
         gather(0, 3)
         quantize_x(0)
-        gather(1, 0)
         gather(1, 1)
         gather(2, 0)
         gather(2, 1)
@@ -161,27 +199,30 @@ def tile_routed_moe_kernel(tc, xT, w, gate, offs, out):
         gather(3, 2)
         gather(3, 3)
         quantize_x(3)
-        piece(0, 0, 0, 4, "S")
-        piece(0, 1, 0, 4, "S")
-        piece(0, 2, 0, 1, "V")
-        piece(0, 2, 1, 2, "S")
-        piece(0, 2, 2, 4, "S")
-        piece(0, 3, 0, 1, "V")
-        piece(0, 3, 1, 2, "S")
-        way_back(0, 0)
-        piece(0, 3, 2, 3, "V")
-        way_back(0, 1)
-        piece(0, 3, 3, 4, "S")
-        way_back(0, 2)
-        way_back(0, 3)
-        piece(1, 0, 0, 4, "S")
-        piece(1, 1, 0, 4, "S")
-        piece(1, 2, 0, 2, "S")
-        piece(1, 2, 2, 4, "S")
-        piece(1, 3, 0, 1, "V")
-        piece(1, 3, 1, 2, "S")
-        way_back(1, 0)
-        piece(1, 3, 2, 4, "S")
-        way_back(1, 1)
-        way_back(1, 2)
-        way_back(1, 3)
+        piece(0, 0, 4, "S")
+        piece(1, 0, 1, "V")
+        piece(1, 1, 2, "S")
+        piece(1, 2, 3, "V")
+        piece(1, 3, 4, "S")
+        piece(2, 0, 1, "V")
+        piece(2, 1, 2, "S")
+        piece(2, 2, 3, "V")
+        piece(2, 3, 4, "S")
+        piece(3, 0, 1, "V")
+        piece(3, 1, 2, "S")
+        way_back(0, [0])
+        piece(3, 2, 3, "V")
+        way_back(0, [1])
+        piece(3, 3, 4, "S")
+        half_piece(0, 0, 0, 256)
+        half_piece(0, 1, 0, 256)
+        way_back(0, [2])
+        way_back(0, [3])
+        half_piece(1, 0, 0, 128)
+        half_piece(1, 0, 128, 256)
+        way_back(1, [0])
+        half_piece(1, 1, 0, 128)
+        half_piece(1, 1, 128, 256)
+        way_back(1, [1], slot="raw_half11")
+        way_back(1, [2])
+        way_back(1, [3])

from contextlib import ExitStack

import concourse.mybir as mybir

K, T, E, C, N = 2048, 1024, 2, 256, 512
FLOPS = 2 * K * N * E * C

F32 = mybir.dt.float32
BF16 = mybir.dt.bfloat16
U32 = mybir.dt.uint32
U16 = mybir.dt.uint16
U8 = mybir.dt.uint8
FP8X4 = mybir.dt.float8_e4m3fn_x4
MULT = mybir.AluOpType.mult
COPY = mybir.ActivationFunctionType.Copy

P = 128
PACK = 4
K_PASS = P * PACK
PASSES = K // K_PASS
NB = N // P
SLOTS = E * C
LIST_COLS = C // 16
SCALAR_PLANES = ((1, 0), (1, 1), (1, 2), (1, 3), (2, 2), (2, 3))
HALF = N // 2
PAIR = 2


def tile_routed_moe_kernel(tc, xT, w, gate, offs, out):
    nc = tc.nc
    x_view = xT.rearrange("(g p t) n -> g p t n", p=P, t=PACK)
    w_view = w.rearrange("e (g p j) n -> e g p j n", p=P, j=PACK)
    gate_view = gate.rearrange("(b p) s -> p b s", p=P)

    with ExitStack() as ctx:
        keep = ctx.enter_context(tc.tile_pool(name="keep", bufs=1))
        stage = ctx.enter_context(tc.tile_pool(name="stage", bufs=4))
        psum = ctx.enter_context(tc.psum_pool(name="psum", bufs=1))

        offsets = keep.tile([P, SLOTS // 16], U16, name="offsets")
        nc.sync.dma_start(offsets[:], offs)

        raw_x = [keep.tile([P, PACK, T], F32, name="raw_x%d" % g, align_bytes=256) for g in range(PASSES)]
        raw_w = [keep.tile([P, PACK, N], F32, name="raw_w%d" % g, align_bytes=256) for g in range(PASSES)]
        raw_half = {}
        gate_sb = keep.tile([P, NB, SLOTS], F32, name="gate_sb", align_bytes=256)

        def load_x(g, t0, t1):
            nc.sync.dma_start(raw_x[g][:, t0:t1, :], x_view[g, :, t0:t1, :])

        def load_w(g):
            nc.sync.dma_start(raw_w[g][:], w_view[0, g])

        def load_half(h, q):
            raw = keep.tile([P, PAIR, PACK, HALF], F32, name="raw_half%d%d" % (h, q), tag="raw_half%d%d" % (h, q), align_bytes=256)
            for i in range(PAIR):
                nc.sync.dma_start(raw[:, i, :, :], w_view[1, q * PAIR + i, :, :, h * HALF:(h + 1) * HALF])
            raw_half[(h, q)] = raw

        def load_gate(e, b0, b1):
            nc.sync.dma_start(gate_sb[:, b0:b1, e * C:(e + 1) * C], gate_view[:, b0:b1, e * C:(e + 1) * C])

        load_x(0, 0, 1)
        load_x(0, 1, 2)
        load_x(1, 0, 1)
        load_x(0, 2, 3)
        load_x(0, 3, 4)
        load_x(1, 1, 2)
        load_x(2, 0, 2)
        load_x(1, 2, 4)
        load_x(3, 0, 2)
        load_x(2, 2, 4)
        load_x(3, 2, 4)
        load_w(0)
        load_w(1)
        load_w(2)
        load_w(3)
        load_gate(0, 0, 2)
        load_half(0, 0)
        load_half(0, 1)
        load_gate(0, 2, 4)
        load_half(1, 0)
        load_half(1, 1)
        load_gate(1, 0, 1)
        load_gate(1, 1, 4)

        windows = [keep.tile([P, T], F32, name="window%d" % b, align_bytes=256) for b in range(NB)]
        for b in range(NB):
            nc.vector.memset(windows[b][:], 0.0)

        x_codes = [keep.tile([P, SLOTS], U32, name="x_codes%d" % g, align_bytes=64) for g in range(PASSES)]
        x_scales = [keep.tile([P, SLOTS], U8, name="x_scales%d" % g, align_bytes=64) for g in range(PASSES)]
        x_grouped = [keep.tile([P, SLOTS, PACK], BF16, name="x_grouped%d" % g, align_bytes=64) for g in range(PASSES)]
        w_codes = [keep.tile([P, N], U32, name="w_codes%d" % g, align_bytes=64) for g in range(PASSES)]
        w_scales = [keep.tile([P, N], U8, name="w_scales%d" % g, align_bytes=64) for g in range(PASSES)]
        acc = [[psum.tile([P, C], F32, name="acc%d%d" % (e, b)) for b in range(NB)] for e in range(E)]
        w_grouped = {}

        def gather(g, t):
            if (g, t) in SCALAR_PLANES:
                cast = stage.tile([P, T], BF16, name="x_bf16", bufs=3)
                nc.gpsimd.tensor_copy(out=cast[:], in_=raw_x[g][:, t, :])
                nc.scalar.activation(x_grouped[g][:, :, t], cast[:].indirect(offsets[:]), COPY)
            else:
                nc.vector.tensor_copy(out=x_grouped[g][:, :, t], in_=raw_x[g][:, t, :].indirect(offsets[:]))

        def quantize_x(g):
            nc.vector.quantize_mx(
                out=x_codes[g][:].bitcast(FP8X4),
                scales=x_scales[g][:],
                in_=x_grouped[g][:].rearrange("p c t -> p (c t)"),
            )

        def multiply(e, g, b, codes, scales):
            nc.tensor.matmul_mx(
                out=acc[e][b][:],
                lhsT=codes.bitcast(FP8X4),
                lhsT_scale=scales,
                rhs=x_codes[g][:, e * C:(e + 1) * C].bitcast(FP8X4),
                rhs_scale=x_scales[g][:, e * C:(e + 1) * C],
                start=(g == 0),
                stop=(g == PASSES - 1),
            )

        def piece(g, b0, b1, engine):
            n0, n1 = b0 * P, b1 * P
            if b0 == 0:
                w_grouped[g] = stage.tile([P, N, PACK], BF16, name="w_grouped", tag="grouped%d" % N, bufs=3, align_bytes=64)
            grouped = w_grouped[g]
            if engine == "V":
                nc.vector.tensor_copy(
                    out=grouped[:, n0:n1, :],
                    in_=raw_w[g][:, :, n0:n1].rearrange("p j n -> p n j"),
                )
            else:
                nc.scalar.copy(
                    out=grouped[:, n0:n1, :].rearrange("p (c i) j -> p c j i", i=4),
                    in_=raw_w[g][:, :, n0:n1].rearrange("p j (c i) -> p c j i", i=4),
                )
            nc.vector.quantize_mx(
                out=w_codes[g][:, n0:n1].bitcast(FP8X4),
                scales=w_scales[g][:, n0:n1],
                in_=grouped[:].rearrange("p n j -> p (n j)")[:, n0 * PACK:n1 * PACK],
            )
            for b in range(b0, b1):
                multiply(0, g, b, w_codes[g][:, b * P:(b + 1) * P], w_scales[g][:, b * P:(b + 1) * P])

        def half_piece(h, q, c0, c1):
            width = c1 - c0
            raw = raw_half[(h, q)]
            grouped = stage.tile([P, PAIR, width, PACK], BF16, name="half_grouped", tag="grouped%d" % (PAIR * width), bufs=3, align_bytes=64)
            codes = keep.tile([P, PAIR, width], U32, name="half_codes%d%d%d" % (h, q, c0), align_bytes=64)
            scales = keep.tile([P, PAIR, width], U8, name="half_scales%d%d%d" % (h, q, c0), align_bytes=64)
            nc.scalar.copy(
                out=grouped[:].rearrange("p g (c i) j -> p g c j i", i=4),
                in_=raw[:, :, :, c0:c1].rearrange("p g j (c i) -> p g c j i", i=4),
            )
            nc.vector.quantize_mx(
                out=codes[:].rearrange("p g n -> p (g n)").bitcast(FP8X4),
                scales=scales[:].rearrange("p g n -> p (g n)"),
                in_=grouped[:].rearrange("p g n j -> p (g n j)"),
            )
            for f0 in range(0, width, P):
                b = (h * HALF + c0 + f0) // P
                for i in range(PAIR):
                    multiply(1, q * PAIR + i, b, codes[:, i, f0:f0 + P], scales[:, i, f0:f0 + P])

        def way_back(e, blocks, slot=None):
            name = "sums%d%d" % (e, blocks[0])
            sums = keep.tile([P, len(blocks), C], F32, name=name, tag=slot or name, align_bytes=256)
            for k, b in enumerate(blocks):
                nc.scalar.copy(out=sums[:, k, :], in_=acc[e][b][:])
                nc.vector.tensor_tensor(
                    windows[b][:].indirect(offsets[:, e * LIST_COLS:(e + 1) * LIST_COLS]),
                    sums[:, k, :],
                    gate_sb[:, b, e * C:(e + 1) * C],
                    MULT,
                )
                if e == E - 1:
                    nc.sync.dma_start(out[b * P:(b + 1) * P, :], windows[b][:])

        gather(0, 0)
        gather(0, 1)
        gather(1, 0)
        gather(0, 2)
        gather(0, 3)
        quantize_x(0)
        gather(1, 1)
        gather(2, 0)
        gather(2, 1)
        gather(1, 2)
        gather(1, 3)
        quantize_x(1)
        gather(3, 0)
        gather(3, 1)
        gather(2, 2)
        gather(2, 3)
        quantize_x(2)
        gather(3, 2)
        gather(3, 3)
        quantize_x(3)
        piece(0, 0, 4, "S")
        piece(1, 0, 1, "V")
        piece(1, 1, 2, "S")
        piece(1, 2, 3, "V")
        piece(1, 3, 4, "S")
        piece(2, 0, 1, "V")
        piece(2, 1, 2, "S")
        piece(2, 2, 3, "V")
        piece(2, 3, 4, "S")
        piece(3, 0, 1, "V")
        piece(3, 1, 2, "S")
        way_back(0, [0])
        piece(3, 2, 3, "V")
        way_back(0, [1])
        piece(3, 3, 4, "S")
        half_piece(0, 0, 0, 256)
        half_piece(0, 1, 0, 256)
        way_back(0, [2])
        way_back(0, [3])
        half_piece(1, 0, 0, 128)
        half_piece(1, 0, 128, 256)
        way_back(1, [0])
        half_piece(1, 1, 0, 128)
        half_piece(1, 1, 128, 256)
        way_back(1, [1], slot="raw_half11")
        way_back(1, [2])
        way_back(1, [3])
